import numpy as np
CORES = [1,3,5,9,11,13]
N = 6
R, T = 16384, 256
def entries(a): return a.T.reshape(-1)
def pack(v, P): return np.ascontiguousarray(np.asarray(v, np.int32).reshape(-1, P).T)
def lists(rng, how):
    I = rng.integers(0, N * R, (N, T))
    if how == "alike": I[:] = rng.integers(0, N * R)
    if how == "distinct": I = np.stack([rng.permutation(N * R)[:T] for r in range(N)])
    if how == "hotrank": I = R * int(rng.integers(N)) + rng.integers(0, R, (N, T))
    if how == "own": I = R * np.arange(N).reshape(N, 1) + rng.integers(0, R, (N, T))
    if how == "edge": I = R * rng.integers(0, N, (N, T)) + np.where(rng.random((N, T)) < 0.5, 0, R - 1)
    if how == "few": I = rng.choice(rng.integers(0, N * R, 8), (N, T))
    return {"idx": np.stack([pack(I[r], 16) for r in range(N)])}
def setup_inputs(rng):
    return dict({"gr": rng.standard_normal((N, 128, T), dtype=np.float32)}, **lists(rng, "uniform"))
def setup_inputs_alike(rng):
    d = setup_inputs(rng); d.update(lists(rng, "alike"))
    for k in ("gr",): d[k] = (d[k].astype(np.float32) * 1024.0).astype(d[k].dtype)
    return d
def setup_inputs_distinct(rng):
    d = setup_inputs(rng); d.update(lists(rng, "distinct"))
    for k in ("gr",): d[k] = (d[k].astype(np.float32) * (1 / 1024.0)).astype(d[k].dtype)
    return d
def setup_inputs_edge(rng):
    d = setup_inputs(rng); d.update(lists(rng, "edge"))
    return d
def setup_inputs_few(rng):
    d = setup_inputs(rng); d.update(lists(rng, "few"))
    return d
def setup_inputs_hotrank(rng):
    d = setup_inputs(rng); d.update(lists(rng, "hotrank"))
    return d
def check_inputs(x):
    bad = []
    if x["idx"].min() < 0 or x["idx"].max() >= N * R: bad.append("idx out of range")
    return bad
def reference(gr, idx):
    A = np.zeros((128, N * R))
    for r in range(N):
        np.add.at(A.T, entries(idx[r]), gr[r].astype(np.float64).T)
    return {"y": np.stack([A[:, R * r:R * r + R] for r in range(N)]).astype(np.float32)}

@@ -1,0 +1,276 @@
+from concourse.bass import DstId, RemoteDMATransfer
+from concourse.mybir import AluOpType, AxisListType, ActivationFunctionType
+
+N = 6
+R = 16384
+L = 256
+PW = L + 16
+WT = L + R + L
+SIM = 16
+
+SCRATCH = {
+    "img": ("sbuf", [128, WT], "float32"),
+    "grs": ("sbuf", [128, L], "float32"),
+    "grT": ("sbuf", [128, L], "float32"),
+    "idxO": ("sbuf", [128, 16], "int32"),
+    "Dd": ("sbuf", [128, 128], "int32"),
+    "Dm": ("sbuf", [128, 128], "int32"),
+    "Qq": ("sbuf", [128, 16], "int32"),
+    "Qs": ("sbuf", [128, 16], "int32"),
+    "Ak": ("sbuf", [128, 16], "int32"),
+    "Ab": ("sbuf", [128, 16], "int32"),
+    "Bq": ("sbuf", [128, 16], "int32"),
+    "ident": ("sbuf", [128, 128], "float32"),
+    "ltri": ("sbuf", [128, 128], "float32"),
+    "p1": ("sbuf", [128, 128], "float32"),
+    "ones": ("sbuf", [128, 128], "float32"),
+    "p2x": ("sbuf", [128, 16], "float32"),
+    "lo": ("sbuf", [128, 16], "float32"),
+    "hir": ("sbuf", [128, 16], "float32"),
+    "lor": ("sbuf", [128, 16], "float32"),
+    "sh": ("sbuf", [128, 16], "int32"),
+    "sh2": ("sbuf", [128, 16], "float32"),
+    "kO": ("sbuf", [128, 16], "float32"),
+    "tA": ("sbuf", [128, 16], "float32"),
+    "col": ("sbuf", [128, 4], "float32"),
+    "diag": ("sbuf", [128, L], "float32"),
+    "S0": ("sbuf", [128, L], "float32"),
+    "S1": ("sbuf", [128, L], "float32"),
+    "sl": ("sbuf", [128, L], "float32"),
+    "cn": ("sbuf", [128, 4], "float32"),
+    "fl": ("sbuf", [128, 4], "float32"),
+    "rhsK": ("sbuf", [128, 16], "float32"),
+    "pay": ("sbuf", [128, PW], "float32"),
+    "land": ("sbuf", [128, N * PW], "float32"),
+    "m1": ("sbuf", [128, 16], "float32"),
+    "m2": ("sbuf", [128, 16], "float32"),
+    "offs": ("sbuf", [128, 16 * N], "uint16"),
+    "tmp": ("sbuf", [128, L], "float32"),
+    "psB": ("psum", [128, 512], "float32"),
+    "psT0": ("psum", [128, 512], "float32"),
+    "psT1": ("psum", [128, 512], "float32"),
+    "psG": ("psum", [128, 512], "float32"),
+    "psK": ("psum", [128, 512], "float32"),
+}
+SEMAPHORES = ["vc", "pc", "sc", "gc", "ldi", "ldg", "zd", "ys", "sent"] + ["arr%d" % s for s in range(N)]
+
+
+def _bits(m):
+    return [e for e in range(32) if (m >> e) & 1]
+
+
+def _mask(bl):
+    v = 0
+    for e in bl:
+        v |= 1 << e
+    return v
+
+
+def _routes(T, topo):
+    cores = list(T.cores)
+    used = []
+    out = []
+    for c in cores:
+        peers = [d for d in cores if d != c and topo.chip(d) == topo.chip(c)]
+        far = [d for d in cores if topo.chip(d) != topo.chip(c)]
+        relay = None
+        if far and not all(topo.may_write(c, d) for d in far):
+            cand = [h for h in range(SIM) if h not in cores and h not in used and topo.chip(h) == topo.chip(c)
+                    and all(topo.may_write(h, d) for d in far)]
+            same = [h for h in cand if topo.die(h) == topo.die(c)]
+            relay = (same or cand)[0]
+            used.append(relay)
+        out.append({"core": c, "peers": peers, "far": far, "relay": relay})
+    return out
+
+
+def _transfer(T, topo, s, src_ap, dsts, mask):
+    ids = []
+    for d in dsts:
+        rid, pid, _se = topo.addr(d)
+        ids.append(DstId(rid=rid, pnc=pid))
+    slot = T.land[:, s * PW:(s + 1) * PW]
+    return RemoteDMATransfer(dst_ids=ids, dma_engine_mask=mask, remote_sem=T.sem["arr%d" % s],
+                             srcs=[src_ap], dsts=[slot for d in dsts])
+
+
+def _far_mask(topo, c, far):
+    m = topo.mask(c, far[0])
+    for d in far:
+        m &= topo.mask(c, d)
+    return m
+
+
+def rank_program(g, core, T, topo):
+    routes = _routes(T, topo)
+    sem = T.sem
+    rank = T.rank_of(core)
+
+    if rank is None:
+        for s, rt in enumerate(routes):
+            if rt["relay"] == core:
+                n_in = len(_bits(topo.mask(rt["core"], core)))
+                fm = _far_mask(topo, core, rt["far"])
+                g.wait_ge(sem["arr%d" % s], n_in)
+                g.remote_dma_fused([_transfer(T, topo, s, T.land[:, s * PW:(s + 1) * PW], rt["far"], fm)],
+                                   local_sem=sem.sent)
+                g.wait_ge(sem.sent, len(_bits(fm)))
+        return
+
+    V, PE, A, SY = g.vector, g.tensor, g.scalar, g.sync
+    op = AluOpType
+    cnt = {"vc": 0, "pc": 0, "sc": 0, "gc": 0}
+    queue = {"vc": V, "pc": PE, "sc": A, "gc": g}
+
+    def step(ch, fn, waits=()):
+        q = queue[ch]
+        for (nm, n) in waits:
+            q.wait_ge(sem[nm], n)
+        if cnt[ch]:
+            q.wait_ge(sem[ch], cnt[ch])
+        fn().then_inc(sem[ch], 1)
+        cnt[ch] += 1
+        return (ch, cnt[ch])
+
+    def v(fn, waits=()):
+        return step("vc", fn, waits)
+
+    def ts(out, in0, s1, s2, o0, o1=None):
+        if o1 is None:
+            return lambda: V.tensor_scalar(out, in0, s1, None, o0)
+        return lambda: V.tensor_scalar(out, in0, s1, s2, o0, o1)
+
+    def tt(out, a, b, o):
+        return lambda: V.tensor_tensor(out, a, b, o)
+
+    img = T.img
+    SEED = 512
+    z_sc = [(1024 + 1024 * i, 2048 + 1024 * i) for i in range(8)]
+    z_g = (9216, 11776)
+    z_d = [(11776 + 512 * i, 12288 + 512 * i) for i in range(4)]
+    z_v = [(13824, 14592), (14592, 15360), (15360, WT)]
+
+    for grp in range(8):
+        q = SY if grp < 4 else A
+        q.dma_start(T.idxO[16 * grp:16 * grp + 16, :], T.idx[:, :]).then_inc(sem.ldi, 16)
+    SY.dma_start(T.grs[:, :], T.gr[:, :]).then_inc(sem.ldg, 16)
+    LDI = ("ldi", 128)
+    LDG = ("ldg", 16)
+
+    gD = step("gc", lambda: g.iota(T.Dd[:, :], [[-1, 128]], 0, 1))
+    gQ = step("gc", lambda: g.iota(T.Qq[:, :], [[0, 2], [-16, 8]], 0, 1))
+    gA = step("gc", lambda: g.iota(T.Ak[:, :], [[0, 16]], 0, 1))
+    gB = step("gc", lambda: g.iota(T.Bq[:, :], [[16, 16]], 0, 0))
+    gZ = step("gc", lambda: g.iota(img[:, z_g[0]:z_g[1]], [[0, z_g[1] - z_g[0]]], 0, 0,
+                                   allow_small_or_imprecise_dtypes=True))
+
+    vSeed = v(lambda: V.memset(img[:, 0:SEED], 0.0))
+    v(lambda: V.memset(T.ones[:, :], 1.0))
+    vId = v(ts(T.ident[:, :], T.Dd[:, :], 0, None, op.is_equal), [gD])
+    v(ts(T.Qs[:, :], T.Qq[:, :], 4, None, op.arith_shift_right), [gQ])
+    v(ts(T.p2x[:, :], T.Qs[:, :], 0, None, op.is_equal))
+    v(ts(T.ltri[:, :], T.Dd[:, :], 0, None, op.is_gt))
+    v(ts(T.Dm[:, :], T.Dd[:, :], 15, None, op.bitwise_and))
+    v(ts(T.p1[:, :], T.Dm[:, :], 0, None, op.is_equal))
+    v(ts(T.Ab[:, :], T.Ak[:, :], 15, None, op.bitwise_and), [gA])
+    v(tt(T.lo[:, :], T.Ab[:, :], T.Bq[:, :], op.add), [gB])
+    base = -768.0 - 65536.0 * rank
+    v(ts(T.hir[:, :], T.lo[:, :], float(L + R) - base, None, op.add))
+    v(ts(T.lor[:, :], T.lo[:, :], -base, None, op.add))
+
+    step("sc", lambda: A.activation(img[:, SEED:2 * SEED], img[:, 0:SEED], ActivationFunctionType.Copy), [vSeed])
+    for (a, b) in z_sc:
+        sZ = step("sc", lambda a=a, b=b: A.activation(img[:, a:b], img[:, 0:1024], ActivationFunctionType.Copy))
+    SY.wait_ge(sem.vc, vSeed[1])
+    for (a, b) in z_d:
+        SY.dma_start(img[:, a:b], img[:, 0:SEED]).then_inc(sem.zd, 16)
+    ZD = ("zd", 16 * len(z_d))
+
+    v(ts(T.sh[:, :], T.idxO[:, :], 14, None, op.arith_shift_right), [LDI])
+    v(ts(T.sh2[:, :], T.sh[:, :], 49152.0, 1024.0, op.mult, op.add))
+    v(tt(T.kO[:, :], T.sh2[:, :], T.idxO[:, :], op.add))
+    v(tt(T.tA[:, :], T.kO[:, :], T.p2x[:, :], op.mult))
+    for c in range(2):
+        v(lambda c=c: V.tensor_reduce(T.col[:, c:c + 1], T.tA[:, 8 * c:8 * c + 8], AxisListType.X, op.add))
+    vDg = []
+    for c in range(2):
+        vDg.append(v(ts(T.diag[:, 128 * c:128 * c + 128], T.ident[:, :], T.col[:, c:c + 1], None, op.mult)))
+
+    for c in range(2):
+        pB = step("pc", lambda c=c: PE.matmul(T.psB[:, 128 * c:128 * c + 128], T.ones[:, :],
+                                              T.diag[:, 128 * c:128 * c + 128], True, True), [vDg[c]])
+    pT0 = step("pc", lambda: PE.transpose(T.psT0[:, 0:128], T.grs[:, 0:128], T.ident[:, :]), [LDG, vId])
+    pT1 = step("pc", lambda: PE.transpose(T.psT1[:, 0:128], T.grs[:, 128:256], T.ident[:, :]))
+
+    v(lambda: V.memset(img[:, z_v[0][0]:z_v[0][1]], 0.0))
+    vS0 = v(ts(T.S0[:, :], T.psB[:, 0:L], T.col[:, 0:1], None, op.is_equal), [pB])
+    vS1 = v(ts(T.S1[:, :], T.psB[:, 0:L], T.col[:, 1:2], None, op.is_equal))
+    vT0 = v(lambda: V.tensor_copy(T.grT[:, 0:128], T.psT0[:, 0:128]), [pT0])
+    v(tt(T.sl[:, 0:128], T.S0[:, 0:128], T.ltri[:, :], op.mult))
+    vT1 = v(lambda: V.tensor_copy(T.grT[:, 128:256], T.psT1[:, 0:128]), [pT1])
+
+    step("pc", lambda: PE.matmul(T.psG[:, 0:L], T.grT[:, 0:128], T.S0[:, :], True, False), [vS0, vT0])
+    pG = step("pc", lambda: PE.matmul(T.psG[:, 0:L], T.grT[:, 128:256], T.S1[:, :], False, True), [vS1, vT1])
+
+    v(tt(T.sl[:, 128:256], T.S1[:, 128:256], T.ltri[:, :], op.mult))
+    v(lambda: V.tensor_reduce(T.cn[:, 0:1], T.sl[:, 0:128], AxisListType.X, op.add))
+    v(lambda: V.tensor_reduce(T.cn[:, 2:3], T.S1[:, 0:128], AxisListType.X, op.add))
+    v(lambda: V.tensor_reduce(T.cn[:, 3:4], T.sl[:, 128:256], AxisListType.X, op.add))
+    v(tt(T.cn[:, 1:2], T.cn[:, 2:3], T.cn[:, 3:4], op.add))
+    v(ts(T.fl[:, 0:2], T.cn[:, 0:2], 0.0, None, op.is_equal))
+    for c in range(2):
+        vK = v(ts(T.rhsK[:, 8 * c:8 * c + 8], T.p2x[:, 0:8], T.fl[:, c:c + 1], T.col[:, c:c + 1], op.mult, op.mult))
+    pK = step("pc", lambda: PE.matmul(T.psK[:, 0:16], T.p1[:, :], T.rhsK[:, :], True, True), [vK])
+
+    v(lambda: V.memset(img[:, z_v[1][0]:z_v[1][1]], 0.0))
+    v(lambda: V.tensor_copy(T.pay[:, 0:L], T.psG[:, 0:L]), [pG])
+    vPay = v(lambda: V.tensor_copy(T.pay[:, L:PW], T.psK[:, 0:16]), [pK])
+
+    rt = routes[rank]
+    g.wait_ge(sem.vc, vPay[1])
+    if rt["relay"] is None:
+        fm = _far_mask(topo, core, rt["far"])
+        nm = _mask([e for e in _bits(topo.mask(core, rt["peers"][0])) if e not in _bits(fm)])
+        trs = [_transfer(T, topo, rank, T.pay[:, :], rt["far"], fm), _transfer(T, topo, rank, T.pay[:, :], rt["peers"], nm)]
+        n_sent = len(_bits(fm)) + len(_bits(nm))
+    else:
+        nm = topo.mask(core, rt["relay"])
+        trs = [_transfer(T, topo, rank, T.pay[:, :], [rt["relay"]] + rt["peers"], nm)]
+        n_sent = len(_bits(nm))
+    g.remote_dma_fused(trs, local_sem=sem.sent)
+    g.wait_ge(sem.sent, n_sent)
+
+    def arrives(s):
+        r2 = routes[s]
+        if core in r2["peers"]:
+            if r2["relay"] is None:
+                fm2 = _far_mask(topo, r2["core"], r2["far"])
+                return len([e for e in _bits(topo.mask(r2["core"], core)) if e not in _bits(fm2)])
+            return len(_bits(topo.mask(r2["core"], r2["relay"])))
+        carrier = r2["core"] if r2["relay"] is None else r2["relay"]
+        return len(_bits(_far_mask(topo, carrier, r2["far"])))
+
+    def offsets(s, key, waits=()):
+        v(tt(T.m1[:, :], key, T.hir[:, :], op.min), waits)
+        v(tt(T.m2[:, :], T.m1[:, :], T.lor[:, :], op.max))
+        v(ts(T.offs[:, 16 * s:16 * s + 16], T.m2[:, :], base, None, op.add))
+
+    offsets(rank, T.pay[:, L:PW])
+    v(lambda: V.memset(img[:, z_v[2][0]:z_v[2][1]], 0.0))
+    last = v(lambda: V.tensor_copy(img[:, 0:WT].indirect(T.offs[:, 16 * rank:16 * rank + 16]), T.pay[:, 0:L]),
+             [sZ, gZ, ZD])
+    order = [s for s in range(N) if core in routes[s]["peers"]]
+    order += [s for s in range(N) if core in routes[s]["far"] and routes[s]["relay"] is None]
+    order += [s for s in range(N) if core in routes[s]["far"] and routes[s]["relay"] is not None]
+    for s in order:
+        o = T.offs[:, 16 * s:16 * s + 16]
+        offsets(s, T.land[:, s * PW + L:(s + 1) * PW], [("arr%d" % s, arrives(s))])
+        v(tt(T.tmp[:, :], img[:, 0:WT].indirect(o), T.land[:, s * PW:s * PW + L], op.add))
+        last = v(lambda o=o: V.tensor_copy(img[:, 0:WT].indirect(o), T.tmp[:, :]))
+
+    H = R // 2
+    SY.wait_ge(sem.vc, last[1])
+    SY.dma_start(T.y[:, 0:H], img[:, L:L + H]).then_inc(sem.ys, 16)
+    A.wait_ge(sem.vc, last[1])
+    A.dma_start(T.y[:, H:R], img[:, L + H:L + R]).then_inc(sem.ys, 16)
+    SY.wait_ge(sem.ys, 32)

@@ -4,9 +4,11 @@ from concourse.mybir import AluOpType, AxisListType, ActivationFunctionType
 N = 6
 R = 16384
 L = 256
-PW = L + 16
+PW = L
 WT = L + R + L
 SIM = 16
+ZB = 512
+Z_H = (12544, 15104)
 
 SCRATCH = {
     "img": ("sbuf", [128, WT], "float32"),
@@ -17,17 +19,17 @@ SCRATCH = {
     "Dm": ("sbuf", [128, 128], "int32"),
     "Qq": ("sbuf", [128, 16], "int32"),
     "Qs": ("sbuf", [128, 16], "int32"),
-    "Ak": ("sbuf", [128, 16], "int32"),
-    "Ab": ("sbuf", [128, 16], "int32"),
-    "Bq": ("sbuf", [128, 16], "int32"),
+    "Ak": ("sbuf", [128, 16 * N], "int32"),
+    "Ab": ("sbuf", [128, 16 * N], "int32"),
+    "Bq": ("sbuf", [128, 16 * N], "int32"),
     "ident": ("sbuf", [128, 128], "float32"),
     "ltri": ("sbuf", [128, 128], "float32"),
     "p1": ("sbuf", [128, 128], "float32"),
     "ones": ("sbuf", [128, 128], "float32"),
     "p2x": ("sbuf", [128, 16], "float32"),
-    "lo": ("sbuf", [128, 16], "float32"),
-    "hir": ("sbuf", [128, 16], "float32"),
-    "lor": ("sbuf", [128, 16], "float32"),
+    "lo": ("sbuf", [128, 16 * N], "float32"),
+    "hir": ("sbuf", [128, 16 * N], "float32"),
+    "lor": ("sbuf", [128, 16 * N], "float32"),
     "sh": ("sbuf", [128, 16], "int32"),
     "sh2": ("sbuf", [128, 16], "float32"),
     "kO": ("sbuf", [128, 16], "float32"),
@@ -42,17 +44,20 @@ SCRATCH = {
     "rhsK": ("sbuf", [128, 16], "float32"),
     "pay": ("sbuf", [128, PW], "float32"),
     "land": ("sbuf", [128, N * PW], "float32"),
-    "m1": ("sbuf", [128, 16], "float32"),
-    "m2": ("sbuf", [128, 16], "float32"),
+    "keyt": ("sbuf", [128, 16 * N], "float32"),
+    "m1": ("sbuf", [128, 16 * N], "float32"),
+    "m2": ("sbuf", [128, 16 * N], "float32"),
     "offs": ("sbuf", [128, 16 * N], "uint16"),
     "tmp": ("sbuf", [128, L], "float32"),
+    "zt": ("sbuf", [128, ZB], "float32"),
     "psB": ("psum", [128, 512], "float32"),
     "psT0": ("psum", [128, 512], "float32"),
     "psT1": ("psum", [128, 512], "float32"),
     "psG": ("psum", [128, 512], "float32"),
     "psK": ("psum", [128, 512], "float32"),
 }
-SEMAPHORES = ["vc", "pc", "sc", "gc", "ldi", "ldg", "zd", "ys", "sent"] + ["arr%d" % s for s in range(N)]
+SEMAPHORES = (["vc", "pc", "sc", "gc", "ldi", "ldg", "zd", "zr", "ys", "sent"] + ["arr%d" % s for s in range(N)]
+              + ["karr%d" % s for s in range(N)])
 
 
 def _bits(m):
@@ -68,30 +73,61 @@ def _mask(bl):
 
 def _routes(T, topo):
     cores = list(T.cores)
-    used = []
     out = []
     for c in cores:
-        peers = [d for d in cores if d != c and topo.chip(d) == topo.chip(c)]
+        mine = [d for d in cores if topo.chip(d) == topo.chip(c)]
+        at = mine.index(c)
+        peers = mine[at + 1:] + mine[:at]
         far = [d for d in cores if topo.chip(d) != topo.chip(c)]
-        relay = None
-        if far and not all(topo.may_write(c, d) for d in far):
-            cand = [h for h in range(SIM) if h not in cores and h not in used and topo.chip(h) == topo.chip(c)
-                    and all(topo.may_write(h, d) for d in far)]
-            same = [h for h in cand if topo.die(h) == topo.die(c)]
-            relay = (same or cand)[0]
-            used.append(relay)
-        out.append({"core": c, "peers": peers, "far": far, "relay": relay})
+        own = all(topo.may_write(c, d) for d in far)
+        out.append({"core": c, "peers": peers, "far": far, "own": own, "carry": [(c, far)] if own else []})
+    for ch in sorted({topo.chip(c) for c in cores}):
+        need = [rt for rt in out if topo.chip(rt["core"]) == ch and not rt["own"]]
+        free = [h for h in range(SIM) if h not in cores and topo.chip(h) == ch
+                and all(topo.may_write(h, d) for rt in need for d in rt["far"])]
+        first = {}
+        for rt in need:
+            same = [h for h in free if topo.die(h) == topo.die(rt["core"])]
+            first[rt["core"]] = (same or free)[0]
+            free.remove(first[rt["core"]])
+        for rt in need:
+            if free and len(rt["far"]) > 1:
+                rt["carry"] = [(first[rt["core"]], rt["far"][:-1]), (free[0], rt["far"][-1:])]
+            else:
+                rt["carry"] = [(first[rt["core"]], rt["far"])]
     return out
 
 
-def _transfer(T, topo, s, src_ap, dsts, mask):
+def _order(routes, core):
+    own = [s for s, rt in enumerate(routes) if rt["core"] == core]
+    early = sorted([s for s, rt in enumerate(routes) if core in rt["peers"]], key=lambda s: routes[s]["peers"].index(core))
+    early += [s for s, rt in enumerate(routes) if core in rt["far"] and rt["own"]]
+    late = [s for s, rt in enumerate(routes) if core in rt["far"] and not rt["own"]]
+    return own, early, late
+
+
+def _kslot(T, routes, d, s):
+    if T.rank_of(d) is None:
+        return s
+    own, early, late = _order(routes, d)
+    return (own + early + late).index(s)
+
+
+def _ids(topo, dsts):
     ids = []
     for d in dsts:
         rid, pid, _se = topo.addr(d)
         ids.append(DstId(rid=rid, pnc=pid))
-    slot = T.land[:, s * PW:(s + 1) * PW]
-    return RemoteDMATransfer(dst_ids=ids, dma_engine_mask=mask, remote_sem=T.sem["arr%d" % s],
-                             srcs=[src_ap], dsts=[slot for d in dsts])
+    return ids
+
+
+def _transfer(T, topo, routes, s, kind, src_ap, dsts, mask):
+    if kind == "k":
+        aps = [T.keyt[:, 16 * _kslot(T, routes, d, s):16 * _kslot(T, routes, d, s) + 16] for d in dsts]
+        sm = T.sem["karr%d" % s]
+    else:
+        aps, sm = [T.land[:, s * PW:(s + 1) * PW] for d in dsts], T.sem["arr%d" % s]
+    return RemoteDMATransfer(dst_ids=_ids(topo, dsts), dma_engine_mask=mask, remote_sem=sm, srcs=[src_ap], dsts=aps)
 
 
 def _far_mask(topo, c, far):
@@ -101,20 +137,53 @@ def _far_mask(topo, c, far):
     return m
 
 
+def _zero_jobs(T, topo, routes):
+    cores = list(T.cores)
+    jobs = {}
+    for ch in sorted({topo.chip(c) for c in cores}):
+        ranks = [c for c in cores if topo.chip(c) == ch]
+        idle = [h for h in range(SIM) if h not in cores and topo.chip(h) == ch]
+        for h in idle:
+            m = topo.mask(h, ranks[0])
+            for rt in routes:
+                for (hh, far) in rt["carry"]:
+                    if hh == h:
+                        m = _mask([e for e in _bits(m) if e not in _bits(_far_mask(topo, h, far))])
+            jobs[h] = (m, [])
+        for b in range((Z_H[1] - Z_H[0]) // ZB):
+            for c in ranks:
+                h = min(idle, key=lambda x: (len(jobs[x][1]) + 1.0) / len(_bits(jobs[x][0])))
+                jobs[h][1].append((c, b))
+    return jobs
+
+
 def rank_program(g, core, T, topo):
     routes = _routes(T, topo)
+    zjobs = _zero_jobs(T, topo, routes)
     sem = T.sem
     rank = T.rank_of(core)
 
     if rank is None:
-        for s, rt in enumerate(routes):
-            if rt["relay"] == core:
+        total = 0
+        zm, zl = zjobs.get(core, (0, []))
+        if zl:
+            g.vector.memset(T.zt[:, :], 0.0).then_inc(sem.vc, 1)
+            g.wait_ge(sem.vc, 1)
+            aps = [T.img[:, Z_H[0] + ZB * b:Z_H[0] + ZB * (b + 1)] for (c, b) in zl]
+            g.remote_dma_fused([RemoteDMATransfer(dst_ids=_ids(topo, [c for (c, b) in zl]), dma_engine_mask=zm,
+                                                  remote_sem=sem.zr, srcs=[T.zt[:, :]], dsts=aps)], local_sem=sem.sent)
+            total += len(_bits(zm))
+        jobs = [(s, rt, far) for s, rt in enumerate(routes) for (h, far) in rt["carry"] if h == core]
+        for kind in ("k", "v"):
+            for (s, rt, far) in jobs:
                 n_in = len(_bits(topo.mask(rt["core"], core)))
-                fm = _far_mask(topo, core, rt["far"])
-                g.wait_ge(sem["arr%d" % s], n_in)
-                g.remote_dma_fused([_transfer(T, topo, s, T.land[:, s * PW:(s + 1) * PW], rt["far"], fm)],
-                                   local_sem=sem.sent)
-                g.wait_ge(sem.sent, len(_bits(fm)))
+                fm = _far_mask(topo, core, far)
+                src = T.keyt[:, 16 * s:16 * s + 16] if kind == "k" else T.land[:, s * PW:(s + 1) * PW]
+                g.wait_ge(sem[("karr%d" if kind == "k" else "arr%d") % s], n_in)
+                g.remote_dma_fused([_transfer(T, topo, routes, s, kind, src, far, fm)], local_sem=sem.sent)
+                total += len(_bits(fm))
+        if total:
+            g.wait_ge(sem.sent, total)
         return
 
     V, PE, A, SY = g.vector, g.tensor, g.scalar, g.sync
@@ -145,10 +214,11 @@ def rank_program(g, core, T, topo):
 
     img = T.img
     SEED = 512
-    z_sc = [(1024 + 1024 * i, 2048 + 1024 * i) for i in range(8)]
-    z_g = (9216, 11776)
-    z_d = [(11776 + 512 * i, 12288 + 512 * i) for i in range(4)]
-    z_v = [(13824, 14592), (14592, 15360), (15360, WT)]
+    z_sc = [(1024 + 1024 * i, 2048 + 1024 * i) for i in range(5)] + [(6144, 6912)]
+    z_g = (6912, 9472)
+    z_d = [(9472 + 512 * i, 9984 + 512 * i) for i in range(6)]
+    z_v = [(15104, 15616), (15616, 16128), (16128, WT)]
+    ZR = ("zr", sum(len(_bits(m)) for (m, zl) in zjobs.values() for (c, b) in zl if c == core))
 
     for grp in range(8):
         q = SY if grp < 4 else A
@@ -159,8 +229,8 @@ def rank_program(g, core, T, topo):
 
     gD = step("gc", lambda: g.iota(T.Dd[:, :], [[-1, 128]], 0, 1))
     gQ = step("gc", lambda: g.iota(T.Qq[:, :], [[0, 2], [-16, 8]], 0, 1))
-    gA = step("gc", lambda: g.iota(T.Ak[:, :], [[0, 16]], 0, 1))
-    gB = step("gc", lambda: g.iota(T.Bq[:, :], [[16, 16]], 0, 0))
+    gA = step("gc", lambda: g.iota(T.Ak[:, :], [[0, 16 * N]], 0, 1))
+    gB = step("gc", lambda: g.iota(T.Bq[:, :], [[0, N], [16, 16]], 0, 0))
     gZ = step("gc", lambda: g.iota(img[:, z_g[0]:z_g[1]], [[0, z_g[1] - z_g[0]]], 0, 0,
                                    allow_small_or_imprecise_dtypes=True))
 
@@ -169,18 +239,12 @@ def rank_program(g, core, T, topo):
     vId = v(ts(T.ident[:, :], T.Dd[:, :], 0, None, op.is_equal), [gD])
     v(ts(T.Qs[:, :], T.Qq[:, :], 4, None, op.arith_shift_right), [gQ])
     v(ts(T.p2x[:, :], T.Qs[:, :], 0, None, op.is_equal))
-    v(ts(T.ltri[:, :], T.Dd[:, :], 0, None, op.is_gt))
-    v(ts(T.Dm[:, :], T.Dd[:, :], 15, None, op.bitwise_and))
-    v(ts(T.p1[:, :], T.Dm[:, :], 0, None, op.is_equal))
-    v(ts(T.Ab[:, :], T.Ak[:, :], 15, None, op.bitwise_and), [gA])
-    v(tt(T.lo[:, :], T.Ab[:, :], T.Bq[:, :], op.add), [gB])
+    v(lambda: V.memset(img[:, z_v[0][0]:z_v[0][1]], 0.0))
     base = -768.0 - 65536.0 * rank
-    v(ts(T.hir[:, :], T.lo[:, :], float(L + R) - base, None, op.add))
-    v(ts(T.lor[:, :], T.lo[:, :], -base, None, op.add))
 
     step("sc", lambda: A.activation(img[:, SEED:2 * SEED], img[:, 0:SEED], ActivationFunctionType.Copy), [vSeed])
     for (a, b) in z_sc:
-        sZ = step("sc", lambda a=a, b=b: A.activation(img[:, a:b], img[:, 0:1024], ActivationFunctionType.Copy))
+        sZ = step("sc", lambda a=a, b=b: A.activation(img[:, a:b], img[:, 0:b - a], ActivationFunctionType.Copy))
     SY.wait_ge(sem.vc, vSeed[1])
     for (a, b) in z_d:
         SY.dma_start(img[:, a:b], img[:, 0:SEED]).then_inc(sem.zd, 16)
@@ -202,7 +266,10 @@ def rank_program(g, core, T, topo):
     pT0 = step("pc", lambda: PE.transpose(T.psT0[:, 0:128], T.grs[:, 0:128], T.ident[:, :]), [LDG, vId])
     pT1 = step("pc", lambda: PE.transpose(T.psT1[:, 0:128], T.grs[:, 128:256], T.ident[:, :]))
 
-    v(lambda: V.memset(img[:, z_v[0][0]:z_v[0][1]], 0.0))
+    v(ts(T.ltri[:, :], T.Dd[:, :], 0, None, op.is_gt))
+    v(ts(T.Dm[:, :], T.Dd[:, :], 15, None, op.bitwise_and))
+    v(ts(T.p1[:, :], T.Dm[:, :], 0, None, op.is_equal))
+    v(lambda: V.memset(img[:, z_v[1][0]:z_v[1][1]], 0.0))
     vS0 = v(ts(T.S0[:, :], T.psB[:, 0:L], T.col[:, 0:1], None, op.is_equal), [pB])
     vS1 = v(ts(T.S1[:, :], T.psB[:, 0:L], T.col[:, 1:2], None, op.is_equal))
     vT0 = v(lambda: V.tensor_copy(T.grT[:, 0:128], T.psT0[:, 0:128]), [pT0])
@@ -210,7 +277,6 @@ def rank_program(g, core, T, topo):
     vT1 = v(lambda: V.tensor_copy(T.grT[:, 128:256], T.psT1[:, 0:128]), [pT1])
 
     step("pc", lambda: PE.matmul(T.psG[:, 0:L], T.grT[:, 0:128], T.S0[:, :], True, False), [vS0, vT0])
-    pG = step("pc", lambda: PE.matmul(T.psG[:, 0:L], T.grT[:, 128:256], T.S1[:, :], False, True), [vS1, vT1])
 
     v(tt(T.sl[:, 128:256], T.S1[:, 128:256], T.ltri[:, :], op.mult))
     v(lambda: V.tensor_reduce(T.cn[:, 0:1], T.sl[:, 0:128], AxisListType.X, op.add))
@@ -221,52 +287,63 @@ def rank_program(g, core, T, topo):
     for c in range(2):
         vK = v(ts(T.rhsK[:, 8 * c:8 * c + 8], T.p2x[:, 0:8], T.fl[:, c:c + 1], T.col[:, c:c + 1], op.mult, op.mult))
     pK = step("pc", lambda: PE.matmul(T.psK[:, 0:16], T.p1[:, :], T.rhsK[:, :], True, True), [vK])
+    pG = step("pc", lambda: PE.matmul(T.psG[:, 0:L], T.grT[:, 128:256], T.S1[:, :], False, True), [vS1, vT1])
 
-    v(lambda: V.memset(img[:, z_v[1][0]:z_v[1][1]], 0.0))
-    v(lambda: V.tensor_copy(T.pay[:, 0:L], T.psG[:, 0:L]), [pG])
-    vPay = v(lambda: V.tensor_copy(T.pay[:, L:PW], T.psK[:, 0:16]), [pK])
+    v(ts(T.Ab[:, :], T.Ak[:, :], 15, None, op.bitwise_and), [gA])
+    v(tt(T.lo[:, :], T.Ab[:, :], T.Bq[:, :], op.add), [gB])
+    v(ts(T.hir[:, :], T.lo[:, :], float(L + R) - base, None, op.add))
+    v(ts(T.lor[:, :], T.lo[:, :], -base, None, op.add))
+    mykey = T.keyt[:, 0:16]
+    vKey = v(lambda: V.tensor_copy(mykey, T.psK[:, 0:16]), [pK])
+    v(lambda: V.memset(img[:, z_v[2][0]:z_v[2][1]], 0.0))
+    vPay = v(lambda: V.tensor_copy(T.pay[:, 0:L], T.psG[:, 0:L]), [pG])
 
     rt = routes[rank]
-    g.wait_ge(sem.vc, vPay[1])
-    if rt["relay"] is None:
-        fm = _far_mask(topo, core, rt["far"])
-        nm = _mask([e for e in _bits(topo.mask(core, rt["peers"][0])) if e not in _bits(fm)])
-        trs = [_transfer(T, topo, rank, T.pay[:, :], rt["far"], fm), _transfer(T, topo, rank, T.pay[:, :], rt["peers"], nm)]
-        n_sent = len(_bits(fm)) + len(_bits(nm))
-    else:
-        nm = topo.mask(core, rt["relay"])
-        trs = [_transfer(T, topo, rank, T.pay[:, :], [rt["relay"]] + rt["peers"], nm)]
-        n_sent = len(_bits(nm))
-    g.remote_dma_fused(trs, local_sem=sem.sent)
+    n_sent = 0
+    for kind, src, ready in (("k", mykey, vKey), ("v", T.pay[:, :], vPay)):
+        g.wait_ge(sem.vc, ready[1])
+        if rt["own"]:
+            fm = _far_mask(topo, core, rt["far"])
+            nm = _mask([e for e in _bits(topo.mask(core, rt["peers"][0])) if e not in _bits(fm)])
+            trs = [_transfer(T, topo, routes, rank, kind, src, rt["far"], fm),
+                   _transfer(T, topo, routes, rank, kind, src, rt["peers"], nm)]
+            n_sent += len(_bits(fm)) + len(_bits(nm))
+        else:
+            hs = [h for (h, far) in rt["carry"]]
+            nm = topo.mask(core, hs[0])
+            trs = [_transfer(T, topo, routes, rank, kind, src, rt["peers"] + hs, nm)]
+            n_sent += len(_bits(nm))
+        g.remote_dma_fused(trs, local_sem=sem.sent)
     g.wait_ge(sem.sent, n_sent)
 
     def arrives(s):
         r2 = routes[s]
         if core in r2["peers"]:
-            if r2["relay"] is None:
+            if r2["own"]:
                 fm2 = _far_mask(topo, r2["core"], r2["far"])
                 return len([e for e in _bits(topo.mask(r2["core"], core)) if e not in _bits(fm2)])
-            return len(_bits(topo.mask(r2["core"], r2["relay"])))
-        carrier = r2["core"] if r2["relay"] is None else r2["relay"]
-        return len(_bits(_far_mask(topo, carrier, r2["far"])))
+            return len(_bits(topo.mask(r2["core"], core)))
+        for (h, far) in r2["carry"]:
+            if core in far:
+                return len(_bits(_far_mask(topo, h, far)))
 
-    def offsets(s, key, waits=()):
-        v(tt(T.m1[:, :], key, T.hir[:, :], op.min), waits)
-        v(tt(T.m2[:, :], T.m1[:, :], T.lor[:, :], op.max))
-        v(ts(T.offs[:, 16 * s:16 * s + 16], T.m2[:, :], base, None, op.add))
+    def offsets(a, n, waits=()):
+        c0, c1 = 16 * a, 16 * (a + n)
+        v(tt(T.m1[:, c0:c1], T.keyt[:, c0:c1], T.hir[:, c0:c1], op.min), waits)
+        v(tt(T.m2[:, c0:c1], T.m1[:, c0:c1], T.lor[:, c0:c1], op.max))
+        v(ts(T.offs[:, c0:c1], T.m2[:, c0:c1], base, None, op.add))
 
-    offsets(rank, T.pay[:, L:PW])
-    v(lambda: V.memset(img[:, z_v[2][0]:z_v[2][1]], 0.0))
-    last = v(lambda: V.tensor_copy(img[:, 0:WT].indirect(T.offs[:, 16 * rank:16 * rank + 16]), T.pay[:, 0:L]),
-             [sZ, gZ, ZD])
-    order = [s for s in range(N) if core in routes[s]["peers"]]
-    order += [s for s in range(N) if core in routes[s]["far"] and routes[s]["relay"] is None]
-    order += [s for s in range(N) if core in routes[s]["far"] and routes[s]["relay"] is not None]
-    for s in order:
-        o = T.offs[:, 16 * s:16 * s + 16]
-        offsets(s, T.land[:, s * PW + L:(s + 1) * PW], [("arr%d" % s, arrives(s))])
-        v(tt(T.tmp[:, :], img[:, 0:WT].indirect(o), T.land[:, s * PW:s * PW + L], op.add))
-        last = v(lambda o=o: V.tensor_copy(img[:, 0:WT].indirect(o), T.tmp[:, :]))
+    own, early, late = _order(routes, core)
+    offsets(0, 1)
+    last = v(lambda: V.tensor_copy(img[:, 0:WT].indirect(T.offs[:, 0:16]), T.pay[:, 0:L]), [sZ, gZ, ZD, ZR])
+    place = 1
+    for group in (early, late):
+        offsets(place, len(group), [("karr%d" % s, arrives(s)) for s in group])
+        for s in group:
+            o = T.offs[:, 16 * place:16 * place + 16]
+            place += 1
+            v(tt(T.tmp[:, :], img[:, 0:WT].indirect(o), T.land[:, s * PW:s * PW + L], op.add), [("arr%d" % s, arrives(s))])
+            last = v(lambda o=o: V.tensor_copy(img[:, 0:WT].indirect(o), T.tmp[:, :]))
 
     H = R // 2
     SY.wait_ge(sem.vc, last[1])

@@ -8,7 +8,7 @@ PW = L
 WT = L + R + L
 SIM = 16
 ZB = 512
-Z_H = (12544, 15104)
+Z_H = (11776, 16384)
 
 SCRATCH = {
     "img": ("sbuf", [128, WT], "float32"),
@@ -50,10 +50,12 @@ SCRATCH = {
     "offs": ("sbuf", [128, 16 * N], "uint16"),
     "tmp": ("sbuf", [128, L], "float32"),
     "zt": ("sbuf", [128, ZB], "float32"),
-    "psB": ("psum", [128, 512], "float32"),
+    "psB0": ("psum", [128, 512], "float32"),
+    "psB1": ("psum", [128, 512], "float32"),
     "psT0": ("psum", [128, 512], "float32"),
     "psT1": ("psum", [128, 512], "float32"),
-    "psG": ("psum", [128, 512], "float32"),
+    "psG0": ("psum", [128, 512], "float32"),
+    "psG1": ("psum", [128, 512], "float32"),
     "psK": ("psum", [128, 512], "float32"),
 }
 SEMAPHORES = (["vc", "pc", "sc", "gc", "ldi", "ldg", "zd", "zr", "ys", "sent"] + ["arr%d" % s for s in range(N)]
@@ -144,12 +146,7 @@ def _zero_jobs(T, topo, routes):
         ranks = [c for c in cores if topo.chip(c) == ch]
         idle = [h for h in range(SIM) if h not in cores and topo.chip(h) == ch]
         for h in idle:
-            m = topo.mask(h, ranks[0])
-            for rt in routes:
-                for (hh, far) in rt["carry"]:
-                    if hh == h:
-                        m = _mask([e for e in _bits(m) if e not in _bits(_far_mask(topo, h, far))])
-            jobs[h] = (m, [])
+            jobs[h] = (topo.mask(h, ranks[0]), [])
         for b in range((Z_H[1] - Z_H[0]) // ZB):
             for c in ranks:
                 h = min(idle, key=lambda x: (len(jobs[x][1]) + 1.0) / len(_bits(jobs[x][0])))
@@ -214,16 +211,16 @@ def rank_program(g, core, T, topo):
 
     img = T.img
     SEED = 512
-    z_sc = [(1024 + 1024 * i, 2048 + 1024 * i) for i in range(5)] + [(6144, 6912)]
-    z_g = (6912, 9472)
-    z_d = [(9472 + 512 * i, 9984 + 512 * i) for i in range(6)]
-    z_v = [(15104, 15616), (15616, 16128), (16128, WT)]
+    z_sc = [(1024 + 1024 * i, 2048 + 1024 * i) for i in range(5)]
+    z_g = (6144, 8192)
+    z_d = [(8192 + 512 * i, 8704 + 512 * i) for i in range(7)]
+    z_v = (16384, WT)
     ZR = ("zr", sum(len(_bits(m)) for (m, zl) in zjobs.values() for (c, b) in zl if c == core))
 
-    for grp in range(8):
-        q = SY if grp < 4 else A
-        q.dma_start(T.idxO[16 * grp:16 * grp + 16, :], T.idx[:, :]).then_inc(sem.ldi, 16)
     SY.dma_start(T.grs[:, :], T.gr[:, :]).then_inc(sem.ldg, 16)
+    for grp in range(8):
+        q = A if grp < 4 else SY
+        q.dma_start(T.idxO[16 * grp:16 * grp + 16, :], T.idx[:, :]).then_inc(sem.ldi, 16)
     LDI = ("ldi", 128)
     LDG = ("ldg", 16)
 
@@ -239,7 +236,7 @@ def rank_program(g, core, T, topo):
     vId = v(ts(T.ident[:, :], T.Dd[:, :], 0, None, op.is_equal), [gD])
     v(ts(T.Qs[:, :], T.Qq[:, :], 4, None, op.arith_shift_right), [gQ])
     v(ts(T.p2x[:, :], T.Qs[:, :], 0, None, op.is_equal))
-    v(lambda: V.memset(img[:, z_v[0][0]:z_v[0][1]], 0.0))
+    v(lambda: V.memset(img[:, z_v[0]:z_v[1]], 0.0))
     base = -768.0 - 65536.0 * rank
 
     step("sc", lambda: A.activation(img[:, SEED:2 * SEED], img[:, 0:SEED], ActivationFunctionType.Copy), [vSeed])
@@ -260,23 +257,25 @@ def rank_program(g, core, T, topo):
     for c in range(2):
         vDg.append(v(ts(T.diag[:, 128 * c:128 * c + 128], T.ident[:, :], T.col[:, c:c + 1], None, op.mult)))
 
-    for c in range(2):
-        pB = step("pc", lambda c=c: PE.matmul(T.psB[:, 128 * c:128 * c + 128], T.ones[:, :],
-                                              T.diag[:, 128 * c:128 * c + 128], True, True), [vDg[c]])
     pT0 = step("pc", lambda: PE.transpose(T.psT0[:, 0:128], T.grs[:, 0:128], T.ident[:, :]), [LDG, vId])
     pT1 = step("pc", lambda: PE.transpose(T.psT1[:, 0:128], T.grs[:, 128:256], T.ident[:, :]))
+    pB0 = step("pc", lambda: PE.matmul(T.psB0[:, 0:128], T.ones[:, :], T.diag[:, 0:128], True, True), [vDg[0]])
+    pB1 = step("pc", lambda: PE.matmul(T.psB1[:, 0:128], T.ones[:, :], T.diag[:, 128:256], True, True), [vDg[1]])
 
+    vT0 = v(lambda: V.tensor_copy(T.grT[:, 0:128], T.psT0[:, 0:128]), [pT0])
     v(ts(T.ltri[:, :], T.Dd[:, :], 0, None, op.is_gt))
     v(ts(T.Dm[:, :], T.Dd[:, :], 15, None, op.bitwise_and))
     v(ts(T.p1[:, :], T.Dm[:, :], 0, None, op.is_equal))
-    v(lambda: V.memset(img[:, z_v[1][0]:z_v[1][1]], 0.0))
-    vS0 = v(ts(T.S0[:, :], T.psB[:, 0:L], T.col[:, 0:1], None, op.is_equal), [pB])
-    vS1 = v(ts(T.S1[:, :], T.psB[:, 0:L], T.col[:, 1:2], None, op.is_equal))
-    vT0 = v(lambda: V.tensor_copy(T.grT[:, 0:128], T.psT0[:, 0:128]), [pT0])
-    v(tt(T.sl[:, 0:128], T.S0[:, 0:128], T.ltri[:, :], op.mult))
+    v(ts(T.Ab[:, :], T.Ak[:, :], 15, None, op.bitwise_and), [gA])
     vT1 = v(lambda: V.tensor_copy(T.grT[:, 128:256], T.psT1[:, 0:128]), [pT1])
+    vS00 = v(ts(T.S0[:, 0:128], T.psB0[:, 0:128], T.col[:, 0:1], None, op.is_equal), [pB0])
+    vS10 = v(ts(T.S1[:, 0:128], T.psB0[:, 0:128], T.col[:, 1:2], None, op.is_equal))
+    v(tt(T.sl[:, 0:128], T.S0[:, 0:128], T.ltri[:, :], op.mult))
+    vS11 = v(ts(T.S1[:, 128:256], T.psB1[:, 0:128], T.col[:, 1:2], None, op.is_equal), [pB1])
 
-    step("pc", lambda: PE.matmul(T.psG[:, 0:L], T.grT[:, 0:128], T.S0[:, :], True, False), [vS0, vT0])
+    step("pc", lambda: PE.matmul(T.psG0[:, 0:128], T.grT[:, 0:128], T.S0[:, 0:128], True, False), [vS00, vT0])
+    pG0 = step("pc", lambda: PE.matmul(T.psG0[:, 0:128], T.grT[:, 128:256], T.S1[:, 0:128], False, True), [vS10, vT1])
+    pG1 = step("pc", lambda: PE.matmul(T.psG1[:, 0:128], T.grT[:, 128:256], T.S1[:, 128:256], True, True), [vS11])
 
     v(tt(T.sl[:, 128:256], T.S1[:, 128:256], T.ltri[:, :], op.mult))
     v(lambda: V.tensor_reduce(T.cn[:, 0:1], T.sl[:, 0:128], AxisListType.X, op.add))
@@ -287,20 +286,16 @@ def rank_program(g, core, T, topo):
     for c in range(2):
         vK = v(ts(T.rhsK[:, 8 * c:8 * c + 8], T.p2x[:, 0:8], T.fl[:, c:c + 1], T.col[:, c:c + 1], op.mult, op.mult))
     pK = step("pc", lambda: PE.matmul(T.psK[:, 0:16], T.p1[:, :], T.rhsK[:, :], True, True), [vK])
-    pG = step("pc", lambda: PE.matmul(T.psG[:, 0:L], T.grT[:, 128:256], T.S1[:, :], False, True), [vS1, vT1])
 
-    v(ts(T.Ab[:, :], T.Ak[:, :], 15, None, op.bitwise_and), [gA])
+    v(lambda: V.tensor_copy(T.pay[:, 0:128], T.psG0[:, 0:128]), [pG0])
     v(tt(T.lo[:, :], T.Ab[:, :], T.Bq[:, :], op.add), [gB])
     v(ts(T.hir[:, :], T.lo[:, :], float(L + R) - base, None, op.add))
     v(ts(T.lor[:, :], T.lo[:, :], -base, None, op.add))
-    mykey = T.keyt[:, 0:16]
-    vKey = v(lambda: V.tensor_copy(mykey, T.psK[:, 0:16]), [pK])
-    v(lambda: V.memset(img[:, z_v[2][0]:z_v[2][1]], 0.0))
-    vPay = v(lambda: V.tensor_copy(T.pay[:, 0:L], T.psG[:, 0:L]), [pG])
+    vPay = v(lambda: V.tensor_copy(T.pay[:, 128:256], T.psG1[:, 0:128]), [pG1])
 
     rt = routes[rank]
     n_sent = 0
-    for kind, src, ready in (("k", mykey, vKey), ("v", T.pay[:, :], vPay)):
+    for kind, src, ready in (("k", T.rhsK[:, :], vK), ("v", T.pay[:, :], vPay)):
         g.wait_ge(sem.vc, ready[1])
         if rt["own"]:
             fm = _far_mask(topo, core, rt["far"])
@@ -327,18 +322,24 @@ def rank_program(g, core, T, topo):
             if core in far:
                 return len(_bits(_far_mask(topo, h, far)))
 
-    def offsets(a, n, waits=()):
+    def offsets(bank, a, n, pk):
         c0, c1 = 16 * a, 16 * (a + n)
-        v(tt(T.m1[:, c0:c1], T.keyt[:, c0:c1], T.hir[:, c0:c1], op.min), waits)
+        v(tt(T.m1[:, c0:c1], bank[:, 0:16 * n], T.hir[:, c0:c1], op.min), [pk])
         v(tt(T.m2[:, c0:c1], T.m1[:, c0:c1], T.lor[:, c0:c1], op.max))
         v(ts(T.offs[:, c0:c1], T.m2[:, c0:c1], base, None, op.add))
 
     own, early, late = _order(routes, core)
-    offsets(0, 1)
+    near = [s for s in early if core in routes[s]["peers"]]
+    farl = [s for s in early if s not in near] + late
+    offsets(T.psK, 0, 1, pK)
     last = v(lambda: V.tensor_copy(img[:, 0:WT].indirect(T.offs[:, 0:16]), T.pay[:, 0:L]), [sZ, gZ, ZD, ZR])
     place = 1
-    for group in (early, late):
-        offsets(place, len(group), [("karr%d" % s, arrives(s)) for s in group])
+    for group, bank in ((near, T.psT0), (farl, T.psT1)):
+        n = len(group)
+        pk = step("pc", lambda bank=bank, n=n, place=place: PE.matmul(bank[:, 0:16 * n], T.p1[:, :],
+                                                                      T.keyt[:, 16 * place:16 * (place + n)], True, True),
+                  [("karr%d" % s, arrives(s)) for s in group])
+        offsets(bank, place, n, pk)
         for s in group:
             o = T.offs[:, 16 * place:16 * place + 16]
             place += 1

from concourse.bass import DstId, RemoteDMATransfer
from concourse.mybir import AluOpType, AxisListType, ActivationFunctionType

N = 6
R = 16384
L = 256
PW = L
WT = L + R + L
SIM = 16
ZB = 512
Z_H = (11776, 16384)

SCRATCH = {
    "img": ("sbuf", [128, WT], "float32"),
    "grs": ("sbuf", [128, L], "float32"),
    "grT": ("sbuf", [128, L], "float32"),
    "idxO": ("sbuf", [128, 16], "int32"),
    "Dd": ("sbuf", [128, 128], "int32"),
    "Dm": ("sbuf", [128, 128], "int32"),
    "Qq": ("sbuf", [128, 16], "int32"),
    "Qs": ("sbuf", [128, 16], "int32"),
    "Ak": ("sbuf", [128, 16 * N], "int32"),
    "Ab": ("sbuf", [128, 16 * N], "int32"),
    "Bq": ("sbuf", [128, 16 * N], "int32"),
    "ident": ("sbuf", [128, 128], "float32"),
    "ltri": ("sbuf", [128, 128], "float32"),
    "p1": ("sbuf", [128, 128], "float32"),
    "ones": ("sbuf", [128, 128], "float32"),
    "p2x": ("sbuf", [128, 16], "float32"),
    "lo": ("sbuf", [128, 16 * N], "float32"),
    "hir": ("sbuf", [128, 16 * N], "float32"),
    "lor": ("sbuf", [128, 16 * N], "float32"),
    "sh": ("sbuf", [128, 16], "int32"),
    "sh2": ("sbuf", [128, 16], "float32"),
    "kO": ("sbuf", [128, 16], "float32"),
    "tA": ("sbuf", [128, 16], "float32"),
    "col": ("sbuf", [128, 4], "float32"),
    "diag": ("sbuf", [128, L], "float32"),
    "S0": ("sbuf", [128, L], "float32"),
    "S1": ("sbuf", [128, L], "float32"),
    "sl": ("sbuf", [128, L], "float32"),
    "cn": ("sbuf", [128, 4], "float32"),
    "fl": ("sbuf", [128, 4], "float32"),
    "rhsK": ("sbuf", [128, 16], "float32"),
    "pay": ("sbuf", [128, PW], "float32"),
    "land": ("sbuf", [128, N * PW], "float32"),
    "keyt": ("sbuf", [128, 16 * N], "float32"),
    "m1": ("sbuf", [128, 16 * N], "float32"),
    "m2": ("sbuf", [128, 16 * N], "float32"),
    "offs": ("sbuf", [128, 16 * N], "uint16"),
    "tmp": ("sbuf", [128, L], "float32"),
    "zt": ("sbuf", [128, ZB], "float32"),
    "psB0": ("psum", [128, 512], "float32"),
    "psB1": ("psum", [128, 512], "float32"),
    "psT0": ("psum", [128, 512], "float32"),
    "psT1": ("psum", [128, 512], "float32"),
    "psG0": ("psum", [128, 512], "float32"),
    "psG1": ("psum", [128, 512], "float32"),
    "psK": ("psum", [128, 512], "float32"),
}
SEMAPHORES = (["vc", "pc", "sc", "gc", "ldi", "ldg", "zd", "zr", "ys", "sent"] + ["arr%d" % s for s in range(N)]
              + ["karr%d" % s for s in range(N)])


def _bits(m):
    return [e for e in range(32) if (m >> e) & 1]


def _mask(bl):
    v = 0
    for e in bl:
        v |= 1 << e
    return v


def _routes(T, topo):
    cores = list(T.cores)
    out = []
    for c in cores:
        mine = [d for d in cores if topo.chip(d) == topo.chip(c)]
        at = mine.index(c)
        peers = mine[at + 1:] + mine[:at]
        far = [d for d in cores if topo.chip(d) != topo.chip(c)]
        own = all(topo.may_write(c, d) for d in far)
        out.append({"core": c, "peers": peers, "far": far, "own": own, "carry": [(c, far)] if own else []})
    for ch in sorted({topo.chip(c) for c in cores}):
        need = [rt for rt in out if topo.chip(rt["core"]) == ch and not rt["own"]]
        free = [h for h in range(SIM) if h not in cores and topo.chip(h) == ch
                and all(topo.may_write(h, d) for rt in need for d in rt["far"])]
        first = {}
        for rt in need:
            same = [h for h in free if topo.die(h) == topo.die(rt["core"])]
            first[rt["core"]] = (same or free)[0]
            free.remove(first[rt["core"]])
        for rt in need:
            if free and len(rt["far"]) > 1:
                rt["carry"] = [(first[rt["core"]], rt["far"][:-1]), (free[0], rt["far"][-1:])]
            else:
                rt["carry"] = [(first[rt["core"]], rt["far"])]
    return out


def _order(routes, core):
    own = [s for s, rt in enumerate(routes) if rt["core"] == core]
    early = sorted([s for s, rt in enumerate(routes) if core in rt["peers"]], key=lambda s: routes[s]["peers"].index(core))
    early += [s for s, rt in enumerate(routes) if core in rt["far"] and rt["own"]]
    late = [s for s, rt in enumerate(routes) if core in rt["far"] and not rt["own"]]
    return own, early, late


def _kslot(T, routes, d, s):
    if T.rank_of(d) is None:
        return s
    own, early, late = _order(routes, d)
    return (own + early + late).index(s)


def _ids(topo, dsts):
    ids = []
    for d in dsts:
        rid, pid, _se = topo.addr(d)
        ids.append(DstId(rid=rid, pnc=pid))
    return ids


def _transfer(T, topo, routes, s, kind, src_ap, dsts, mask):
    if kind == "k":
        aps = [T.keyt[:, 16 * _kslot(T, routes, d, s):16 * _kslot(T, routes, d, s) + 16] for d in dsts]
        sm = T.sem["karr%d" % s]
    else:
        aps, sm = [T.land[:, s * PW:(s + 1) * PW] for d in dsts], T.sem["arr%d" % s]
    return RemoteDMATransfer(dst_ids=_ids(topo, dsts), dma_engine_mask=mask, remote_sem=sm, srcs=[src_ap], dsts=aps)


def _far_mask(topo, c, far):
    m = topo.mask(c, far[0])
    for d in far:
        m &= topo.mask(c, d)
    return m


def _zero_jobs(T, topo, routes):
    cores = list(T.cores)
    jobs = {}
    for ch in sorted({topo.chip(c) for c in cores}):
        ranks = [c for c in cores if topo.chip(c) == ch]
        idle = [h for h in range(SIM) if h not in cores and topo.chip(h) == ch]
        for h in idle:
            jobs[h] = (topo.mask(h, ranks[0]), [])
        for b in range((Z_H[1] - Z_H[0]) // ZB):
            for c in ranks:
                h = min(idle, key=lambda x: (len(jobs[x][1]) + 1.0) / len(_bits(jobs[x][0])))
                jobs[h][1].append((c, b))
    return jobs


def rank_program(g, core, T, topo):
    routes = _routes(T, topo)
    zjobs = _zero_jobs(T, topo, routes)
    sem = T.sem
    rank = T.rank_of(core)

    if rank is None:
        total = 0
        zm, zl = zjobs.get(core, (0, []))
        if zl:
            g.vector.memset(T.zt[:, :], 0.0).then_inc(sem.vc, 1)
            g.wait_ge(sem.vc, 1)
            aps = [T.img[:, Z_H[0] + ZB * b:Z_H[0] + ZB * (b + 1)] for (c, b) in zl]
            g.remote_dma_fused([RemoteDMATransfer(dst_ids=_ids(topo, [c for (c, b) in zl]), dma_engine_mask=zm,
                                                  remote_sem=sem.zr, srcs=[T.zt[:, :]], dsts=aps)], local_sem=sem.sent)
            total += len(_bits(zm))
        jobs = [(s, rt, far) for s, rt in enumerate(routes) for (h, far) in rt["carry"] if h == core]
        for kind in ("k", "v"):
            for (s, rt, far) in jobs:
                n_in = len(_bits(topo.mask(rt["core"], core)))
                fm = _far_mask(topo, core, far)
                src = T.keyt[:, 16 * s:16 * s + 16] if kind == "k" else T.land[:, s * PW:(s + 1) * PW]
                g.wait_ge(sem[("karr%d" if kind == "k" else "arr%d") % s], n_in)
                g.remote_dma_fused([_transfer(T, topo, routes, s, kind, src, far, fm)], local_sem=sem.sent)
                total += len(_bits(fm))
        if total:
            g.wait_ge(sem.sent, total)
        return

    V, PE, A, SY = g.vector, g.tensor, g.scalar, g.sync
    op = AluOpType
    cnt = {"vc": 0, "pc": 0, "sc": 0, "gc": 0}
    queue = {"vc": V, "pc": PE, "sc": A, "gc": g}

    def step(ch, fn, waits=()):
        q = queue[ch]
        for (nm, n) in waits:
            q.wait_ge(sem[nm], n)
        if cnt[ch]:
            q.wait_ge(sem[ch], cnt[ch])
        fn().then_inc(sem[ch], 1)
        cnt[ch] += 1
        return (ch, cnt[ch])

    def v(fn, waits=()):
        return step("vc", fn, waits)

    def ts(out, in0, s1, s2, o0, o1=None):
        if o1 is None:
            return lambda: V.tensor_scalar(out, in0, s1, None, o0)
        return lambda: V.tensor_scalar(out, in0, s1, s2, o0, o1)

    def tt(out, a, b, o):
        return lambda: V.tensor_tensor(out, a, b, o)

    img = T.img
    SEED = 512
    z_sc = [(1024 + 1024 * i, 2048 + 1024 * i) for i in range(5)]
    z_g = (6144, 8192)
    z_d = [(8192 + 512 * i, 8704 + 512 * i) for i in range(7)]
    z_v = (16384, WT)
    ZR = ("zr", sum(len(_bits(m)) for (m, zl) in zjobs.values() for (c, b) in zl if c == core))

    SY.dma_start(T.grs[:, :], T.gr[:, :]).then_inc(sem.ldg, 16)
    for grp in range(8):
        q = A if grp < 4 else SY
        q.dma_start(T.idxO[16 * grp:16 * grp + 16, :], T.idx[:, :]).then_inc(sem.ldi, 16)
    LDI = ("ldi", 128)
    LDG = ("ldg", 16)

    gD = step("gc", lambda: g.iota(T.Dd[:, :], [[-1, 128]], 0, 1))
    gQ = step("gc", lambda: g.iota(T.Qq[:, :], [[0, 2], [-16, 8]], 0, 1))
    gA = step("gc", lambda: g.iota(T.Ak[:, :], [[0, 16 * N]], 0, 1))
    gB = step("gc", lambda: g.iota(T.Bq[:, :], [[0, N], [16, 16]], 0, 0))
    gZ = step("gc", lambda: g.iota(img[:, z_g[0]:z_g[1]], [[0, z_g[1] - z_g[0]]], 0, 0,
                                   allow_small_or_imprecise_dtypes=True))

    vSeed = v(lambda: V.memset(img[:, 0:SEED], 0.0))
    v(lambda: V.memset(T.ones[:, :], 1.0))
    vId = v(ts(T.ident[:, :], T.Dd[:, :], 0, None, op.is_equal), [gD])
    v(ts(T.Qs[:, :], T.Qq[:, :], 4, None, op.arith_shift_right), [gQ])
    v(ts(T.p2x[:, :], T.Qs[:, :], 0, None, op.is_equal))
    v(lambda: V.memset(img[:, z_v[0]:z_v[1]], 0.0))
    base = -768.0 - 65536.0 * rank

    step("sc", lambda: A.activation(img[:, SEED:2 * SEED], img[:, 0:SEED], ActivationFunctionType.Copy), [vSeed])
    for (a, b) in z_sc:
        sZ = step("sc", lambda a=a, b=b: A.activation(img[:, a:b], img[:, 0:b - a], ActivationFunctionType.Copy))
    SY.wait_ge(sem.vc, vSeed[1])
    for (a, b) in z_d:
        SY.dma_start(img[:, a:b], img[:, 0:SEED]).then_inc(sem.zd, 16)
    ZD = ("zd", 16 * len(z_d))

    v(ts(T.sh[:, :], T.idxO[:, :], 14, None, op.arith_shift_right), [LDI])
    v(ts(T.sh2[:, :], T.sh[:, :], 49152.0, 1024.0, op.mult, op.add))
    v(tt(T.kO[:, :], T.sh2[:, :], T.idxO[:, :], op.add))
    v(tt(T.tA[:, :], T.kO[:, :], T.p2x[:, :], op.mult))
    for c in range(2):
        v(lambda c=c: V.tensor_reduce(T.col[:, c:c + 1], T.tA[:, 8 * c:8 * c + 8], AxisListType.X, op.add))
    vDg = []
    for c in range(2):
        vDg.append(v(ts(T.diag[:, 128 * c:128 * c + 128], T.ident[:, :], T.col[:, c:c + 1], None, op.mult)))

    pT0 = step("pc", lambda: PE.transpose(T.psT0[:, 0:128], T.grs[:, 0:128], T.ident[:, :]), [LDG, vId])
    pT1 = step("pc", lambda: PE.transpose(T.psT1[:, 0:128], T.grs[:, 128:256], T.ident[:, :]))
    pB0 = step("pc", lambda: PE.matmul(T.psB0[:, 0:128], T.ones[:, :], T.diag[:, 0:128], True, True), [vDg[0]])
    pB1 = step("pc", lambda: PE.matmul(T.psB1[:, 0:128], T.ones[:, :], T.diag[:, 128:256], True, True), [vDg[1]])

    vT0 = v(lambda: V.tensor_copy(T.grT[:, 0:128], T.psT0[:, 0:128]), [pT0])
    v(ts(T.ltri[:, :], T.Dd[:, :], 0, None, op.is_gt))
    v(ts(T.Dm[:, :], T.Dd[:, :], 15, None, op.bitwise_and))
    v(ts(T.p1[:, :], T.Dm[:, :], 0, None, op.is_equal))
    v(ts(T.Ab[:, :], T.Ak[:, :], 15, None, op.bitwise_and), [gA])
    vT1 = v(lambda: V.tensor_copy(T.grT[:, 128:256], T.psT1[:, 0:128]), [pT1])
    vS00 = v(ts(T.S0[:, 0:128], T.psB0[:, 0:128], T.col[:, 0:1], None, op.is_equal), [pB0])
    vS10 = v(ts(T.S1[:, 0:128], T.psB0[:, 0:128], T.col[:, 1:2], None, op.is_equal))
    v(tt(T.sl[:, 0:128], T.S0[:, 0:128], T.ltri[:, :], op.mult))
    vS11 = v(ts(T.S1[:, 128:256], T.psB1[:, 0:128], T.col[:, 1:2], None, op.is_equal), [pB1])

    step("pc", lambda: PE.matmul(T.psG0[:, 0:128], T.grT[:, 0:128], T.S0[:, 0:128], True, False), [vS00, vT0])
    pG0 = step("pc", lambda: PE.matmul(T.psG0[:, 0:128], T.grT[:, 128:256], T.S1[:, 0:128], False, True), [vS10, vT1])
    pG1 = step("pc", lambda: PE.matmul(T.psG1[:, 0:128], T.grT[:, 128:256], T.S1[:, 128:256], True, True), [vS11])

    v(tt(T.sl[:, 128:256], T.S1[:, 128:256], T.ltri[:, :], op.mult))
    v(lambda: V.tensor_reduce(T.cn[:, 0:1], T.sl[:, 0:128], AxisListType.X, op.add))
    v(lambda: V.tensor_reduce(T.cn[:, 2:3], T.S1[:, 0:128], AxisListType.X, op.add))
    v(lambda: V.tensor_reduce(T.cn[:, 3:4], T.sl[:, 128:256], AxisListType.X, op.add))
    v(tt(T.cn[:, 1:2], T.cn[:, 2:3], T.cn[:, 3:4], op.add))
    v(ts(T.fl[:, 0:2], T.cn[:, 0:2], 0.0, None, op.is_equal))
    for c in range(2):
        vK = v(ts(T.rhsK[:, 8 * c:8 * c + 8], T.p2x[:, 0:8], T.fl[:, c:c + 1], T.col[:, c:c + 1], op.mult, op.mult))
    pK = step("pc", lambda: PE.matmul(T.psK[:, 0:16], T.p1[:, :], T.rhsK[:, :], True, True), [vK])

    v(lambda: V.tensor_copy(T.pay[:, 0:128], T.psG0[:, 0:128]), [pG0])
    v(tt(T.lo[:, :], T.Ab[:, :], T.Bq[:, :], op.add), [gB])
    v(ts(T.hir[:, :], T.lo[:, :], float(L + R) - base, None, op.add))
    v(ts(T.lor[:, :], T.lo[:, :], -base, None, op.add))
    vPay = v(lambda: V.tensor_copy(T.pay[:, 128:256], T.psG1[:, 0:128]), [pG1])

    rt = routes[rank]
    n_sent = 0
    for kind, src, ready in (("k", T.rhsK[:, :], vK), ("v", T.pay[:, :], vPay)):
        g.wait_ge(sem.vc, ready[1])
        if rt["own"]:
            fm = _far_mask(topo, core, rt["far"])
            nm = _mask([e for e in _bits(topo.mask(core, rt["peers"][0])) if e not in _bits(fm)])
            trs = [_transfer(T, topo, routes, rank, kind, src, rt["far"], fm),
                   _transfer(T, topo, routes, rank, kind, src, rt["peers"], nm)]
            n_sent += len(_bits(fm)) + len(_bits(nm))
        else:
            hs = [h for (h, far) in rt["carry"]]
            nm = topo.mask(core, hs[0])
            trs = [_transfer(T, topo, routes, rank, kind, src, rt["peers"] + hs, nm)]
            n_sent += len(_bits(nm))
        g.remote_dma_fused(trs, local_sem=sem.sent)
    g.wait_ge(sem.sent, n_sent)

    def arrives(s):
        r2 = routes[s]
        if core in r2["peers"]:
            if r2["own"]:
                fm2 = _far_mask(topo, r2["core"], r2["far"])
                return len([e for e in _bits(topo.mask(r2["core"], core)) if e not in _bits(fm2)])
            return len(_bits(topo.mask(r2["core"], core)))
        for (h, far) in r2["carry"]:
            if core in far:
                return len(_bits(_far_mask(topo, h, far)))

    def offsets(bank, a, n, pk):
        c0, c1 = 16 * a, 16 * (a + n)
        v(tt(T.m1[:, c0:c1], bank[:, 0:16 * n], T.hir[:, c0:c1], op.min), [pk])
        v(tt(T.m2[:, c0:c1], T.m1[:, c0:c1], T.lor[:, c0:c1], op.max))
        v(ts(T.offs[:, c0:c1], T.m2[:, c0:c1], base, None, op.add))

    own, early, late = _order(routes, core)
    near = [s for s in early if core in routes[s]["peers"]]
    farl = [s for s in early if s not in near] + late
    offsets(T.psK, 0, 1, pK)
    last = v(lambda: V.tensor_copy(img[:, 0:WT].indirect(T.offs[:, 0:16]), T.pay[:, 0:L]), [sZ, gZ, ZD, ZR])
    place = 1
    for group, bank in ((near, T.psT0), (farl, T.psT1)):
        n = len(group)
        pk = step("pc", lambda bank=bank, n=n, place=place: PE.matmul(bank[:, 0:16 * n], T.p1[:, :],
                                                                      T.keyt[:, 16 * place:16 * (place + n)], True, True),
                  [("karr%d" % s, arrives(s)) for s in group])
        offsets(bank, place, n, pk)
        for s in group:
            o = T.offs[:, 16 * place:16 * place + 16]
            place += 1
            v(tt(T.tmp[:, :], img[:, 0:WT].indirect(o), T.land[:, s * PW:s * PW + L], op.add), [("arr%d" % s, arrives(s))])
            last = v(lambda o=o: V.tensor_copy(img[:, 0:WT].indirect(o), T.tmp[:, :]))

    H = R // 2
    SY.wait_ge(sem.vc, last[1])
    SY.dma_start(T.y[:, 0:H], img[:, L:L + H]).then_inc(sem.ys, 16)
    A.wait_ge(sem.vc, last[1])
    A.dma_start(T.y[:, H:R], img[:, L + H:L + R]).then_inc(sem.ys, 16)
    SY.wait_ge(sem.ys, 32)
